import numpy as np
import ml_dtypes


def mxq(x, axis, fmt="e4m3"):
    dtype, down = {"e4m3": (ml_dtypes.float8_e4m3fn, 7), "e5m2": (ml_dtypes.float8_e5m2, 14)}[fmt]
    v = np.moveaxis(np.asarray(x, np.float32).astype(ml_dtypes.bfloat16).astype(np.float64), axis, -1)
    blocks = v.reshape(v.shape[:-1] + (-1, 32))
    amax = np.abs(blocks).max(-1, keepdims=True)
    byte = np.maximum(np.where(amax > 0, np.frexp(amax)[1] - 1 + 127, 0) - down, 1)
    scale = np.exp2(byte - 127.0)
    codes = (blocks / scale).astype(np.float32).astype(dtype).astype(np.float64)
    return np.moveaxis((codes * scale).reshape(v.shape), -1, axis)


WIDE = False


def mx_kscale(k):
    if not WIDE:
        return np.ones(k)
    levels = np.array([10, -10, 5, -5, 0])
    if k % 512:
        return np.exp2(np.random.permutation(np.resize(levels, k // 32))).repeat(32)
    a = np.empty((k // 512, 16))
    for p in range(k // 512):
        a[p, :8] = np.random.permutation(np.resize(levels, 8))
        for g in range(8):
            far = levels[np.abs(levels - a[p, g]) >= 10]
            a[p, g + 8] = far[np.random.randint(len(far))]
    return np.exp2(a.ravel()).repeat(32)


def f64(x):
    return np.asarray(x).astype(np.float64)


def striped(idx):
    return np.tile(idx.reshape(-1, 16).T, (8, 1)).astype(np.uint16)


def unstriped(offs):
    return offs[:16].T.reshape(-1).astype(np.int64)


E2M1 = np.array([0.0, 0.5, 1.0, 1.5, 2.0, 3.0, 4.0, 6.0, -0.0, -0.5, -1.0, -1.5, -2.0, -3.0, -4.0, -6.0])


def pack_weight(w, fmt):
    k, n = w.shape
    w = f64(np.asarray(w, np.float32).astype(ml_dtypes.bfloat16)).reshape(k // 32, 32, n)
    amax = np.abs(w).max(1)
    if fmt == "e4m3":
        byte = np.frexp(amax)[1] - 1 + 127 - 7
    else:
        mant, ex = np.frexp(amax / 6.0)
        byte = np.where(mant > 0.5, ex, ex - 1) + 127
    byte = np.clip(np.where(amax > 0, byte, 1), 1, 254)
    scaled = (w * np.exp2(127.0 - byte)[:, None, :]).reshape(k, n).astype(np.float32)
    by_word = np.ascontiguousarray(scaled.reshape(k // 512, 128, 4, n).transpose(0, 1, 3, 2))
    if fmt == "e4m3":
        words = by_word.astype(ml_dtypes.float8_e4m3fn).view(np.uint8)
    else:
        c = by_word.astype(ml_dtypes.float4_e2m1fn).view(np.uint8) & 0xF
        words = (c[..., 0::2] | (c[..., 1::2] << 4)).reshape(k // 512, 128, 2 * n)
    return np.ascontiguousarray(words), np.ascontiguousarray(byte.astype(np.uint8).reshape(k // 512, 16, n))


def unpack_weight(words, scales, fmt):
    g, _, n = scales.shape
    words = np.ascontiguousarray(words).reshape(g, 128, n, -1)
    if fmt == "e4m3":
        vals = words.view(ml_dtypes.float8_e4m3fn).astype(np.float64)
    else:
        nib = np.empty((g, 128, n, 4), np.uint8)
        nib[..., 0::2] = words & 0xF
        nib[..., 1::2] = words >> 4
        vals = E2M1[nib]
    vals = vals * np.repeat(np.exp2(scales.astype(np.float64) - 127.0), 8, axis=1)[..., None]
    return vals.transpose(0, 1, 3, 2).reshape(g * 512, n)


def gelu(v):
    return 0.5 * v * (1.0 + np.tanh(np.sqrt(2.0 / np.pi) * (v + 0.044715 * v**3)))


K, K2, H, N, T, T2, S, P = 1024, 1536, 1024, 512, 4096, 2048, 1024, 512


def setup_inputs():
    n = np.random.standard_normal
    s = mx_kscale(K)[:, None]
    s2 = mx_kscale(K2)[:, None]
    u = mx_kscale(H)[:, None]
    tab_words, tab_scales = pack_weight(n((K, T)) * s, "e4m3")
    tab2_words, tab2_scales = pack_weight(n((K2, T2)) * s2, "e4m3")
    w1 = (n((K, H)) * 0.52 / np.sqrt(K) / s).astype(np.float32)
    gain = (np.exp(0.3 * n(H)) * u[:, 0]).astype(np.float32)
    w2_words, w2_scales = pack_weight(n((H, N)) * 1.9 / np.sqrt(H) / u, "e2m1")
    w3_words, w3_scales = pack_weight(n((K2, N)) / np.sqrt(K2) / s2, "e4m3")
    ward = (0.6 * n(N)).astype(np.float32)
    offs = striped(np.random.permutation(T)[:S])
    offs2 = striped(np.random.permutation(T2)[:P])
    pos1 = striped(np.random.permutation(S)[:P])
    return {"tab_words": tab_words, "tab_scales": tab_scales,
            "tab2_words": tab2_words, "tab2_scales": tab2_scales,
            "w1": w1, "gain": gain, "w2_words": w2_words, "w2_scales": w2_scales,
            "w3_words": w3_words, "w3_scales": w3_scales, "ward": ward,
            "offs": offs, "offs2": offs2, "pos1": pos1}


def reference(tab_words, tab_scales, tab2_words, tab2_scales, w1, gain, w2_words, w2_scales,
              w3_words, w3_scales, ward, offs, offs2, pos1):
    v = unpack_weight(tab_words, tab_scales, "e4m3")[:, unstriped(offs)]
    v2 = unpack_weight(tab2_words, tab2_scales, "e4m3")[:, unstriped(offs2)]
    w2 = unpack_weight(w2_words, w2_scales, "e2m1")
    w3 = unpack_weight(w3_words, w3_scales, "e4m3")
    h = f64(gain)[:, None] * np.sin(mxq(f64(w1), 0, "e4m3").T @ v)
    y = w2.T @ mxq(h, 0, "e4m3")
    b = w3.T @ v2
    joined = np.maximum(y[:, unstriped(pos1)], b)
    return joined + f64(ward)[:, None]

@@ -1,0 +1,264 @@
+from contextlib import ExitStack
+
+import concourse.mybir as mybir
+
+K, K2, H, N, T, T2, S, PICKS = 1024, 1536, 1024, 512, 4096, 2048, 1024, 512
+FLOPS = 2 * (K * H * S + H * N * S + K2 * N * PICKS)
+
+F32 = mybir.dt.float32
+BF16 = mybir.dt.bfloat16
+I32 = mybir.dt.int32
+U32 = mybir.dt.uint32
+U16 = mybir.dt.uint16
+U8 = mybir.dt.uint8
+FP8X4 = mybir.dt.float8_e4m3fn_x4
+FP4X4 = mybir.dt.float4_e2m1fn_x4
+ALU = mybir.AluOpType
+ACT = mybir.ActivationFunctionType
+
+P = 128
+PACK = 4
+PASS = P * PACK
+BANK = 512
+QUADS = 4
+ROWS = 4
+STRIPE = 16
+
+
+def tile_list_deescalation_review_scores_kernel(
+    tc, tab_words, tab_scales, tab2_words, tab2_scales, w1, gain, w2_words, w2_scales,
+    w3_words, w3_scales, ward, offs, offs2, pos1, out,
+):
+    nc = tc.nc
+    k_passes, m_passes, r_passes = K // PASS, K2 // PASS, H // PASS
+    halves, n_tiles = S // BANK, N // P
+
+    with ExitStack() as ctx:
+        keep = ctx.enter_context(tc.tile_pool(name="keep", bufs=1))
+        work = ctx.enter_context(tc.tile_pool(name="work", bufs=2))
+        ring = ctx.enter_context(tc.psum_pool(name="ring", bufs=4))
+        held = ctx.enter_context(tc.psum_pool(name="held", bufs=1))
+
+        def kept(name, shape, dtype):
+            return keep.tile(shape, dtype, name=name, align_bytes=64)
+
+        def entries(offsets, first, count):
+            return offsets[:, first // STRIPE : (first + count) // STRIPE]
+
+        idx = kept("idx", [P, S // STRIPE], U16)
+        idx2 = kept("idx2", [P, PICKS // STRIPE], U16)
+        p1 = kept("p1", [P, PICKS // STRIPE], U16)
+        tab = [kept("tab%d" % a, [P, T], U32) for a in range(k_passes)]
+        tab_sc = kept("tab_sc", [P, T], U8)
+        tab2 = [kept("tab2_%d" % a, [P, T2], U32) for a in range(m_passes)]
+        tab2_sc = kept("tab2_sc", [P, T2], U8)
+        w1_raw = {(b, a): kept("w1_raw%d%d" % (b, a), [P, PACK, PASS], F32)
+                  for b in range(r_passes) for a in range(k_passes)}
+        w1_q = {key: kept("w1_q%d%d" % key, [P, PASS], U32) for key in w1_raw}
+        w1_sc = {key: kept("w1_sc%d%d" % key, [P, PASS], U8) for key in w1_raw}
+        w2_q = kept("w2_q", [P, r_passes, 2 * N], U8)
+        w2_sc = kept("w2_sc", [P, r_passes, N], U8)
+        w3_q = kept("w3_q", [P, m_passes, N], U32)
+        w3_sc = kept("w3_sc", [P, N], U8)
+        v_q = [kept("v_q%d" % a, [P, S], U32) for a in range(k_passes)]
+        v_sc = kept("v_sc", [P, S], U8)
+        v2_q = [kept("v2_q%d" % a, [P, PICKS], U32) for a in range(m_passes)]
+        v2_sc = kept("v2_sc", [P, PICKS], U8)
+        h_q = {(b, c): kept("h_q%d%d" % (b, c), [P, BANK], U32) for b in range(r_passes) for c in range(halves)}
+        h_sc = {key: kept("h_sc%d%d" % key, [P, BANK], U8) for key in h_q}
+        y = [kept("y%d" % u, [P, S], F32) for u in range(n_tiles)]
+        g = kept("g", [P, r_passes * PACK], F32)
+        ward_sb = kept("ward_sb", [P, n_tiles], F32)
+
+        def load_w1(b, a):
+            rows = w1[a * PASS : (a + 1) * PASS, b * PASS : (b + 1) * PASS]
+            nc.sync.dma_start(out=w1_raw[b, a][:], in_=rows.rearrange("(p i) c -> p i c", i=PACK))
+
+        def load_words(dst, words):
+            nc.sync.dma_start(out=dst[:].bitcast(I32), in_=words.rearrange("p t i -> p (t i)").bitcast(I32))
+
+        def load_stacked_scales(dst, scales, queue):
+            passes = scales.shape[0]
+            for quad in range(QUADS):
+                queue.dma_start(
+                    out=dst[32 * quad : 32 * quad + ROWS * passes, :].bitcast(I32),
+                    in_=scales[:, ROWS * quad : ROWS * (quad + 1), :].bitcast(I32))
+
+        for plane in (tab_sc, tab2_sc, w3_sc):
+            nc.vector.memset(plane[:].bitcast(I32), 0)
+        nc.vector.memset(w2_sc[:].rearrange("p a n -> p (a n)").bitcast(I32), 0)
+
+        nc.sync.dma_start(idx[:], offs)
+        nc.sync.dma_start(out=g[:].rearrange("p (b t) -> p b t", t=PACK),
+                          in_=gain.rearrange("(b p t) -> p b t", p=P, t=PACK))
+        load_w1(0, 0)
+        load_stacked_scales(tab_sc, tab_scales, nc.sync)
+        load_w1(0, 1)
+        for a in range(k_passes):
+            load_words(tab[a], tab_words[a])
+        for a in range(k_passes):
+            load_w1(1, a)
+        nc.sync.dma_start(idx2[:], offs2)
+        load_stacked_scales(tab2_sc, tab2_scales, nc.sync)
+        for a in range(m_passes):
+            load_words(tab2[a], tab2_words[a])
+        nc.sync.dma_start(out=w3_q[:].bitcast(I32), in_=w3_words.rearrange("a p c i -> p a (c i)").bitcast(I32))
+        load_stacked_scales(w3_sc, w3_scales, nc.sync)
+        nc.sync.dma_start(out=w2_q[:].bitcast(I32), in_=w2_words.rearrange("a p c -> p a c").bitcast(I32))
+        for quad in range(QUADS):
+            nc.sync.dma_start(
+                out=w2_sc[32 * quad : 32 * quad + ROWS, :, :].bitcast(I32),
+                in_=w2_scales[:, ROWS * quad : ROWS * (quad + 1), :].rearrange("a r n -> r a n").bitcast(I32))
+        nc.sync.dma_start(p1[:], pos1)
+        with nc.allow_non_contiguous_dma(reason="one offset for each partition"):
+            nc.sync.dma_start(out=ward_sb[:], in_=ward.rearrange("(u p) -> p u", p=P))
+
+
+        sign = kept("sign", [P, r_passes * PACK], F32)
+        third = kept("third", [P, r_passes * PACK], F32)
+        three_g = kept("three_g", [P, r_passes * PACK], F32)
+        four_g = kept("four_g", [P, r_passes * PACK], F32)
+        root = kept("root", [P, r_passes * PACK], F32)
+        half = kept("half", [P, r_passes * PACK], F32)
+        nc.vector.memset(half[:], 0.5)
+        nc.vector.tensor_scalar(sign[:], g[:], 0.0, 2.0, ALU.is_ge, ALU.mult)
+        nc.vector.tensor_scalar(sign[:], sign[:], -1.0, None, ALU.add)
+        nc.vector.tensor_scalar(third[:], sign[:], -1.0 / 3.0, None, ALU.mult)
+        nc.vector.scalar_tensor_tensor(three_g[:], g[:], 3.0, sign[:], ALU.mult, ALU.mult)
+        nc.vector.scalar_tensor_tensor(four_g[:], g[:], 4.0, sign[:], ALU.mult, ALU.mult)
+        nc.gpsimd.tensor_tensor(root[:], four_g[:], half[:], ALU.pow)
+
+
+        w1_bf = {}
+
+        def round_w1(b, a, copy):
+            w1_bf[b, a] = work.tile([P, PASS * PACK], BF16, name="w1_bf", align_bytes=64)
+            copy(out=w1_bf[b, a][:].rearrange("p (t m i) -> p m i t", t=PACK, i=PACK),
+                 in_=w1_raw[b, a][:].rearrange("p i (m t) -> p m i t", t=PACK))
+
+        def quantise_w1(b, a):
+            nc.vector.quantize_mx(out=w1_q[b, a][:].bitcast(FP8X4), scales=w1_sc[b, a][:], in_=w1_bf[b, a][:])
+
+        def gather(dst, window, offsets, first, count):
+            nc.vector.tensor_copy(dst[:, first : first + count], window[:].indirect(entries(offsets, first, count)))
+
+        units = [(b, c) for b in range(r_passes) for c in range(halves)]
+        slices = [(b, c, t) for b, c in units for t in range(PACK)]
+        s_tiles, q_tiles, h_rows, h_woven = {}, {}, {}, {}
+
+        def sine(b, c, t):
+            x = ring.tile([P, BANK], F32, name="bank")
+            cols = slice(c * BANK, (c + 1) * BANK)
+            for a in range(k_passes):
+                nc.tensor.matmul_mx(
+                    out=x[:], lhsT=w1_q[b, a][:, t * P : (t + 1) * P].bitcast(FP8X4),
+                    lhsT_scale=w1_sc[b, a][:, t * P : (t + 1) * P],
+                    rhs=v_q[a][:, cols].bitcast(FP8X4), rhs_scale=v_sc[ROWS * a :, cols],
+                    start=(a == 0), stop=(a == k_passes - 1))
+            s_tiles[b, c, t] = work.tile([P, BANK], F32, name="s", bufs=6)
+            col = b * PACK + t
+            nc.scalar.activation(s_tiles[b, c, t][:], x[:], ACT.Sin, scale=third[:, col : col + 1])
+
+        def square(b, c, t):
+            q_tiles[b, c, t] = work.tile([P, BANK], F32, name="q", bufs=6)
+            col = b * PACK + t
+            nc.scalar.activation(q_tiles[b, c, t][:], s_tiles[b, c, t][:], ACT.Square, scale=root[:, col : col + 1])
+
+        def triple(b, c, t):
+            if t == 0:
+                h_rows[b, c] = work.tile([P, PACK, BANK], BF16, name="h_rows", align_bytes=64)
+            col = b * PACK + t
+            nc.vector.scalar_tensor_tensor(h_rows[b, c][:, t, :], q_tiles[b, c, t][:], three_g[:, col : col + 1],
+                                           s_tiles[b, c, t][:], ALU.subtract, ALU.mult)
+
+        def weave(b, c):
+            h_woven[b, c] = work.tile([P, BANK * PACK], BF16, name="h_woven", align_bytes=64)
+            nc.vector.tensor_copy(out=h_woven[b, c][:].rearrange("p (j i t) -> p j t i", i=4, t=PACK),
+                                  in_=h_rows[b, c][:].rearrange("p t (j i) -> p j t i", i=4))
+
+        def quantise_h(b, c):
+            nc.vector.quantize_mx(out=h_q[b, c][:].bitcast(FP8X4), scales=h_sc[b, c][:], in_=h_woven[b, c][:])
+
+        y_banks = {}
+
+        def second_stage(u, c, b):
+            if b == 0:
+                y_banks[u, c] = ring.tile([P, BANK], F32, name="bank")
+            nc.tensor.matmul_mx(
+                out=y_banks[u, c][:], lhsT=w2_q[:, b, 2 * P * u : 2 * P * (u + 1)].bitcast(FP4X4),
+                lhsT_scale=w2_sc[:, b, P * u : P * (u + 1)],
+                rhs=h_q[b, c][:].bitcast(FP8X4), rhs_scale=h_sc[b, c][:],
+                start=(b == 0), stop=(b == r_passes - 1))
+            if b == r_passes - 1:
+                nc.scalar.copy(out=y[u][:, c * BANK : (c + 1) * BANK], in_=y_banks[u, c][:])
+
+        b_banks = [held.tile([P, PICKS], F32, name="b%d" % u) for u in range(n_tiles)]
+
+        def prescriptions(a):
+            gather(v2_q[a], tab2[a], idx2, 0, PICKS)
+            for u in range(n_tiles):
+                nc.tensor.matmul_mx(
+                    out=b_banks[u][:], lhsT=w3_q[:, a, P * u : P * (u + 1)].bitcast(FP8X4),
+                    lhsT_scale=w3_sc[ROWS * a :, P * u : P * (u + 1)],
+                    rhs=v2_q[a][:].bitcast(FP8X4), rhs_scale=v2_sc[ROWS * a :, :],
+                    start=(a == 0), stop=(a == m_passes - 1))
+
+        picked = [kept("picked%d" % u, [P, PICKS], F32) for u in range(n_tiles)]
+        higher = [kept("higher%d" % u, [P, PICKS], F32) for u in range(n_tiles)]
+        result = [kept("result%d" % u, [P, PICKS], F32) for u in range(n_tiles)]
+
+        def join(u, first, count):
+            cols = slice(first, first + count)
+            nc.vector.tensor_tensor(higher[u][:, cols], b_banks[u][:, cols], picked[u][:, cols], ALU.max)
+            nc.scalar.activation(result[u][:, cols], higher[u][:, cols], ACT.Identity, bias=ward_sb[:, u : u + 1])
+            nc.sync.dma_start(out=out[P * u : P * (u + 1), cols], in_=result[u][:, cols])
+
+        gather(v_sc, tab_sc, idx, 0, S)
+        for a in range(k_passes):
+            round_w1(0, a, nc.scalar.copy)
+            quantise_w1(0, a)
+        gather(v_q[0], tab[0], idx, 0, S)
+        for c in range(halves):
+            gather(v_q[1], tab[1], idx, c * BANK, BANK)
+
+        extras = {
+            1: [lambda: round_w1(1, 0, nc.vector.tensor_copy)],
+            3: [lambda: quantise_w1(1, 0)],
+            5: [lambda: round_w1(1, 1, nc.scalar.copy)],
+            7: [lambda: quantise_w1(1, 1), lambda: gather(v2_sc, tab2_sc, idx2, 0, PICKS)],
+            9: [lambda: prescriptions(0)],
+            13: [lambda: prescriptions(1)],
+        }
+        count = len(slices)
+        for step in range(count + 4):
+            if step < count:
+                sine(*slices[step])
+            if 0 <= step - 1 < count:
+                square(*slices[step - 1])
+            if 0 <= step - 2 < count:
+                triple(*slices[step - 2])
+            if step >= 3 and (step - 3) % PACK == PACK - 1:
+                weave(*units[(step - 3) // PACK])
+            if step >= 4 and (step - 4) % PACK == PACK - 1:
+                quantise_h(*units[(step - 4) // PACK])
+            for extra in extras.get(step, []):
+                extra()
+            if step == count:
+                for u in range(n_tiles):
+                    for b in range(r_passes):
+                        second_stage(u, 0, b)
+                for u in range(n_tiles):
+                    second_stage(u, 1, 0)
+        for u in range(n_tiles):
+            second_stage(u, 1, 1)
+        prescriptions(2)
+        last = n_tiles - 1
+        for u in range(last):
+            gather(picked[u], y[u], p1, 0, PICKS)
+            if u > 0:
+                join(u - 1, 0, PICKS)
+        gather(picked[last], y[last], p1, 0, PICKS // 2)
+        join(last - 1, 0, PICKS)
+        gather(picked[last], y[last], p1, PICKS // 2, PICKS // 2)
+        join(last, 0, PICKS // 2)
+        join(last, PICKS // 2, PICKS // 2)

@@ -62,7 +62,7 @@ def tile_list_deescalation_review_scores_kernel(
         w3_sc = kept("w3_sc", [P, N], U8)
         v_q = [kept("v_q%d" % a, [P, S], U32) for a in range(k_passes)]
         v_sc = kept("v_sc", [P, S], U8)
-        v2_q = [kept("v2_q%d" % a, [P, PICKS], U32) for a in range(m_passes)]
+        v2_q = [kept("v2_q%d" % a, [P, PICKS], U32) for a in range(m_passes - 1)]
         v2_sc = kept("v2_sc", [P, PICKS], U8)
         h_q = {(b, c): kept("h_q%d%d" % (b, c), [P, BANK], U32) for b in range(r_passes) for c in range(halves)}
         h_sc = {key: kept("h_sc%d%d" % key, [P, BANK], U8) for key in h_q}
@@ -89,17 +89,17 @@ def tile_list_deescalation_review_scores_kernel(
         nc.vector.memset(w2_sc[:].rearrange("p a n -> p (a n)").bitcast(I32), 0)
 
         nc.sync.dma_start(idx[:], offs)
-        nc.sync.dma_start(out=g[:].rearrange("p (b t) -> p b t", t=PACK),
-                          in_=gain.rearrange("(b p t) -> p b t", p=P, t=PACK))
+        nc.gpsimd.dma_start(out=g[:].rearrange("p (b t) -> p b t", t=PACK),
+                            in_=gain.rearrange("(b p t) -> p b t", p=P, t=PACK))
         load_w1(0, 0)
-        load_stacked_scales(tab_sc, tab_scales, nc.sync)
+        load_stacked_scales(tab_sc, tab_scales, nc.gpsimd)
+        nc.sync.dma_start(idx2[:], offs2)
         load_w1(0, 1)
+        load_stacked_scales(tab2_sc, tab2_scales, nc.gpsimd)
         for a in range(k_passes):
             load_words(tab[a], tab_words[a])
         for a in range(k_passes):
             load_w1(1, a)
-        nc.sync.dma_start(idx2[:], offs2)
-        load_stacked_scales(tab2_sc, tab2_scales, nc.sync)
         for a in range(m_passes):
             load_words(tab2[a], tab2_words[a])
         nc.sync.dma_start(out=w3_q[:].bitcast(I32), in_=w3_words.rearrange("a p c i -> p a (c i)").bitcast(I32))
@@ -172,36 +172,43 @@ def tile_list_deescalation_review_scores_kernel(
                                            s_tiles[b, c, t][:], ALU.subtract, ALU.mult)
 
         def weave(b, c):
-            h_woven[b, c] = work.tile([P, BANK * PACK], BF16, name="h_woven", align_bytes=64)
-            nc.vector.tensor_copy(out=h_woven[b, c][:].rearrange("p (j i t) -> p j t i", i=4, t=PACK),
-                                  in_=h_rows[b, c][:].rearrange("p t (j i) -> p j t i", i=4))
+            if (b, c) == units[-1]:
+                woven = keep.tile([P, BANK * PACK], BF16, tag="last", align_bytes=64)
+            else:
+                woven = work.tile([P, BANK * PACK], BF16, align_bytes=64)
+            h_woven[b, c] = woven
+            split = BANK // 2 if (b, c) == units[-2] else 0
+            for first, end, copy in ((0, split, nc.scalar.copy), (split, BANK, nc.vector.tensor_copy)):
+                if end > first:
+                    copy(out=woven[:, first * PACK : end * PACK].rearrange("p (j i t) -> p j t i", i=4, t=PACK),
+                         in_=h_rows[b, c][:, :, first:end].rearrange("p t (j i) -> p j t i", i=4))
 
         def quantise_h(b, c):
             nc.vector.quantize_mx(out=h_q[b, c][:].bitcast(FP8X4), scales=h_sc[b, c][:], in_=h_woven[b, c][:])
 
-        y_banks = {}
-
-        def second_stage(u, c, b):
-            if b == 0:
-                y_banks[u, c] = ring.tile([P, BANK], F32, name="bank")
-            nc.tensor.matmul_mx(
-                out=y_banks[u, c][:], lhsT=w2_q[:, b, 2 * P * u : 2 * P * (u + 1)].bitcast(FP4X4),
-                lhsT_scale=w2_sc[:, b, P * u : P * (u + 1)],
-                rhs=h_q[b, c][:].bitcast(FP8X4), rhs_scale=h_sc[b, c][:],
-                start=(b == 0), stop=(b == r_passes - 1))
-            if b == r_passes - 1:
-                nc.scalar.copy(out=y[u][:, c * BANK : (c + 1) * BANK], in_=y_banks[u, c][:])
+        def second_stage(u, c):
+            acc = ring.tile([P, BANK], F32, name="bank")
+            for b in range(r_passes):
+                nc.tensor.matmul_mx(
+                    out=acc[:], lhsT=w2_q[:, b, 2 * P * u : 2 * P * (u + 1)].bitcast(FP4X4),
+                    lhsT_scale=w2_sc[:, b, P * u : P * (u + 1)],
+                    rhs=h_q[b, c][:].bitcast(FP8X4), rhs_scale=h_sc[b, c][:],
+                    start=(b == 0), stop=(b == r_passes - 1))
+            nc.scalar.copy(out=y[u][:, c * BANK : (c + 1) * BANK], in_=acc[:])
 
         b_banks = [held.tile([P, PICKS], F32, name="b%d" % u) for u in range(n_tiles)]
+
+        def prescription_pass(u, a):
+            nc.tensor.matmul_mx(
+                out=b_banks[u][:], lhsT=w3_q[:, a, P * u : P * (u + 1)].bitcast(FP8X4),
+                lhsT_scale=w3_sc[ROWS * a :, P * u : P * (u + 1)],
+                rhs=v2_q[a][:].bitcast(FP8X4), rhs_scale=v2_sc[ROWS * a :, :],
+                start=(a == 0), stop=(a == m_passes - 1))
 
         def prescriptions(a):
             gather(v2_q[a], tab2[a], idx2, 0, PICKS)
             for u in range(n_tiles):
-                nc.tensor.matmul_mx(
-                    out=b_banks[u][:], lhsT=w3_q[:, a, P * u : P * (u + 1)].bitcast(FP8X4),
-                    lhsT_scale=w3_sc[ROWS * a :, P * u : P * (u + 1)],
-                    rhs=v2_q[a][:].bitcast(FP8X4), rhs_scale=v2_sc[ROWS * a :, :],
-                    start=(a == 0), stop=(a == m_passes - 1))
+                prescription_pass(u, a)
 
         picked = [kept("picked%d" % u, [P, PICKS], F32) for u in range(n_tiles)]
         higher = [kept("higher%d" % u, [P, PICKS], F32) for u in range(n_tiles)]
@@ -215,8 +222,9 @@ def tile_list_deescalation_review_scores_kernel(
 
         gather(v_sc, tab_sc, idx, 0, S)
         for a in range(k_passes):
-            round_w1(0, a, nc.scalar.copy)
+            round_w1(0, a, nc.vector.tensor_copy)
             quantise_w1(0, a)
+        gather(v2_sc, tab2_sc, idx2, 0, PICKS)
         gather(v_q[0], tab[0], idx, 0, S)
         for c in range(halves):
             gather(v_q[1], tab[1], idx, c * BANK, BANK)
@@ -225,7 +233,7 @@ def tile_list_deescalation_review_scores_kernel(
             1: [lambda: round_w1(1, 0, nc.vector.tensor_copy)],
             3: [lambda: quantise_w1(1, 0)],
             5: [lambda: round_w1(1, 1, nc.scalar.copy)],
-            7: [lambda: quantise_w1(1, 1), lambda: gather(v2_sc, tab2_sc, idx2, 0, PICKS)],
+            7: [lambda: quantise_w1(1, 1)],
             9: [lambda: prescriptions(0)],
             13: [lambda: prescriptions(1)],
         }
@@ -245,13 +253,12 @@ def tile_list_deescalation_review_scores_kernel(
                 extra()
             if step == count:
                 for u in range(n_tiles):
-                    for b in range(r_passes):
-                        second_stage(u, 0, b)
-                for u in range(n_tiles):
-                    second_stage(u, 1, 0)
+                    second_stage(u, 0)
+        v2_q.append(keep.tile([P, PICKS], U32, name="v2_last", tag="last", align_bytes=64))
+        gather(v2_q[2], tab2[2], idx2, 0, PICKS)
         for u in range(n_tiles):
-            second_stage(u, 1, 1)
-        prescriptions(2)
+            second_stage(u, 1)
+            prescription_pass(u, 2)
         last = n_tiles - 1
         for u in range(last):
             gather(picked[u], y[u], p1, 0, PICKS)

@@ -36,8 +36,7 @@ def tile_list_deescalation_review_scores_kernel(
     with ExitStack() as ctx:
         keep = ctx.enter_context(tc.tile_pool(name="keep", bufs=1))
         work = ctx.enter_context(tc.tile_pool(name="work", bufs=2))
-        ring = ctx.enter_context(tc.psum_pool(name="ring", bufs=4))
-        held = ctx.enter_context(tc.psum_pool(name="held", bufs=1))
+        ring = ctx.enter_context(tc.psum_pool(name="ring", bufs=8))
 
         def kept(name, shape, dtype):
             return keep.tile(shape, dtype, name=name, align_bytes=64)
@@ -77,10 +76,10 @@ def tile_list_deescalation_review_scores_kernel(
         def load_words(dst, words):
             nc.sync.dma_start(out=dst[:].bitcast(I32), in_=words.rearrange("p t i -> p (t i)").bitcast(I32))
 
-        def load_stacked_scales(dst, scales, queue):
+        def load_stacked_scales(dst, scales):
             passes = scales.shape[0]
             for quad in range(QUADS):
-                queue.dma_start(
+                nc.sync.dma_start(
                     out=dst[32 * quad : 32 * quad + ROWS * passes, :].bitcast(I32),
                     in_=scales[:, ROWS * quad : ROWS * (quad + 1), :].bitcast(I32))
 
@@ -88,31 +87,31 @@ def tile_list_deescalation_review_scores_kernel(
             nc.vector.memset(plane[:].bitcast(I32), 0)
         nc.vector.memset(w2_sc[:].rearrange("p a n -> p (a n)").bitcast(I32), 0)
 
-        nc.sync.dma_start(idx[:], offs)
-        nc.gpsimd.dma_start(out=g[:].rearrange("p (b t) -> p b t", t=PACK),
-                            in_=gain.rearrange("(b p t) -> p b t", p=P, t=PACK))
         load_w1(0, 0)
-        load_stacked_scales(tab_sc, tab_scales, nc.gpsimd)
-        nc.sync.dma_start(idx2[:], offs2)
+        nc.sync.dma_start(idx[:], offs)
+        nc.sync.dma_start(out=g[:].rearrange("p (b t) -> p b t", t=PACK),
+                          in_=gain.rearrange("(b p t) -> p b t", p=P, t=PACK))
+        load_stacked_scales(tab_sc, tab_scales)
         load_w1(0, 1)
-        load_stacked_scales(tab2_sc, tab2_scales, nc.gpsimd)
         for a in range(k_passes):
             load_words(tab[a], tab_words[a])
         for a in range(k_passes):
             load_w1(1, a)
-        for a in range(m_passes):
+        nc.sync.dma_start(idx2[:], offs2)
+        load_stacked_scales(tab2_sc, tab2_scales)
+        for a in range(m_passes - 1):
             load_words(tab2[a], tab2_words[a])
-        nc.sync.dma_start(out=w3_q[:].bitcast(I32), in_=w3_words.rearrange("a p c i -> p a (c i)").bitcast(I32))
-        load_stacked_scales(w3_sc, w3_scales, nc.sync)
         nc.sync.dma_start(out=w2_q[:].bitcast(I32), in_=w2_words.rearrange("a p c -> p a c").bitcast(I32))
         for quad in range(QUADS):
             nc.sync.dma_start(
                 out=w2_sc[32 * quad : 32 * quad + ROWS, :, :].bitcast(I32),
                 in_=w2_scales[:, ROWS * quad : ROWS * (quad + 1), :].rearrange("a r n -> r a n").bitcast(I32))
+        nc.sync.dma_start(out=w3_q[:].bitcast(I32), in_=w3_words.rearrange("a p c i -> p a (c i)").bitcast(I32))
+        load_stacked_scales(w3_sc, w3_scales)
+        load_words(tab2[m_passes - 1], tab2_words[m_passes - 1])
         nc.sync.dma_start(p1[:], pos1)
         with nc.allow_non_contiguous_dma(reason="one offset for each partition"):
             nc.sync.dma_start(out=ward_sb[:], in_=ward.rearrange("(u p) -> p u", p=P))
-
 
         sign = kept("sign", [P, r_passes * PACK], F32)
         third = kept("third", [P, r_passes * PACK], F32)
@@ -196,19 +195,17 @@ def tile_list_deescalation_review_scores_kernel(
                     start=(b == 0), stop=(b == r_passes - 1))
             nc.scalar.copy(out=y[u][:, c * BANK : (c + 1) * BANK], in_=acc[:])
 
-        b_banks = [held.tile([P, PICKS], F32, name="b%d" % u) for u in range(n_tiles)]
+        b_banks = {}
 
         def prescription_pass(u, a):
+            if a == 0:
+                b_banks[u] = ring.tile([P, PICKS], F32, name="bank")
             nc.tensor.matmul_mx(
                 out=b_banks[u][:], lhsT=w3_q[:, a, P * u : P * (u + 1)].bitcast(FP8X4),
                 lhsT_scale=w3_sc[ROWS * a :, P * u : P * (u + 1)],
                 rhs=v2_q[a][:].bitcast(FP8X4), rhs_scale=v2_sc[ROWS * a :, :],
                 start=(a == 0), stop=(a == m_passes - 1))
 
-        def prescriptions(a):
-            gather(v2_q[a], tab2[a], idx2, 0, PICKS)
-            for u in range(n_tiles):
-                prescription_pass(u, a)
 
         picked = [kept("picked%d" % u, [P, PICKS], F32) for u in range(n_tiles)]
         higher = [kept("higher%d" % u, [P, PICKS], F32) for u in range(n_tiles)]
@@ -224,7 +221,6 @@ def tile_list_deescalation_review_scores_kernel(
         for a in range(k_passes):
             round_w1(0, a, nc.vector.tensor_copy)
             quantise_w1(0, a)
-        gather(v2_sc, tab2_sc, idx2, 0, PICKS)
         gather(v_q[0], tab[0], idx, 0, S)
         for c in range(halves):
             gather(v_q[1], tab[1], idx, c * BANK, BANK)
@@ -233,9 +229,9 @@ def tile_list_deescalation_review_scores_kernel(
             1: [lambda: round_w1(1, 0, nc.vector.tensor_copy)],
             3: [lambda: quantise_w1(1, 0)],
             5: [lambda: round_w1(1, 1, nc.scalar.copy)],
-            7: [lambda: quantise_w1(1, 1)],
-            9: [lambda: prescriptions(0)],
-            13: [lambda: prescriptions(1)],
+            7: [lambda: quantise_w1(1, 1), lambda: gather(v2_sc, tab2_sc, idx2, 0, PICKS)],
+            9: [lambda: gather(v2_q[0], tab2[0], idx2, 0, PICKS)],
+            13: [lambda: gather(v2_q[1], tab2[1], idx2, 0, PICKS)],
         }
         count = len(slices)
         for step in range(count + 4):
@@ -254,6 +250,9 @@ def tile_list_deescalation_review_scores_kernel(
             if step == count:
                 for u in range(n_tiles):
                     second_stage(u, 0)
+                for u in range(n_tiles):
+                    for a in range(m_passes - 1):
+                        prescription_pass(u, a)
         v2_q.append(keep.tile([P, PICKS], U32, name="v2_last", tag="last", align_bytes=64))
         gather(v2_q[2], tab2[2], idx2, 0, PICKS)
         for u in range(n_tiles):

from contextlib import ExitStack

import concourse.mybir as mybir

K, K2, H, N, T, T2, S, PICKS = 1024, 1536, 1024, 512, 4096, 2048, 1024, 512
FLOPS = 2 * (K * H * S + H * N * S + K2 * N * PICKS)

F32 = mybir.dt.float32
BF16 = mybir.dt.bfloat16
I32 = mybir.dt.int32
U32 = mybir.dt.uint32
U16 = mybir.dt.uint16
U8 = mybir.dt.uint8
FP8X4 = mybir.dt.float8_e4m3fn_x4
FP4X4 = mybir.dt.float4_e2m1fn_x4
ALU = mybir.AluOpType
ACT = mybir.ActivationFunctionType

P = 128
PACK = 4
PASS = P * PACK
BANK = 512
QUADS = 4
ROWS = 4
STRIPE = 16


def tile_list_deescalation_review_scores_kernel(
    tc, tab_words, tab_scales, tab2_words, tab2_scales, w1, gain, w2_words, w2_scales,
    w3_words, w3_scales, ward, offs, offs2, pos1, out,
):
    nc = tc.nc
    k_passes, m_passes, r_passes = K // PASS, K2 // PASS, H // PASS
    halves, n_tiles = S // BANK, N // P

    with ExitStack() as ctx:
        keep = ctx.enter_context(tc.tile_pool(name="keep", bufs=1))
        work = ctx.enter_context(tc.tile_pool(name="work", bufs=2))
        ring = ctx.enter_context(tc.psum_pool(name="ring", bufs=8))

        def kept(name, shape, dtype):
            return keep.tile(shape, dtype, name=name, align_bytes=64)

        def entries(offsets, first, count):
            return offsets[:, first // STRIPE : (first + count) // STRIPE]

        idx = kept("idx", [P, S // STRIPE], U16)
        idx2 = kept("idx2", [P, PICKS // STRIPE], U16)
        p1 = kept("p1", [P, PICKS // STRIPE], U16)
        tab = [kept("tab%d" % a, [P, T], U32) for a in range(k_passes)]
        tab_sc = kept("tab_sc", [P, T], U8)
        tab2 = [kept("tab2_%d" % a, [P, T2], U32) for a in range(m_passes)]
        tab2_sc = kept("tab2_sc", [P, T2], U8)
        w1_raw = {(b, a): kept("w1_raw%d%d" % (b, a), [P, PACK, PASS], F32)
                  for b in range(r_passes) for a in range(k_passes)}
        w1_q = {key: kept("w1_q%d%d" % key, [P, PASS], U32) for key in w1_raw}
        w1_sc = {key: kept("w1_sc%d%d" % key, [P, PASS], U8) for key in w1_raw}
        w2_q = kept("w2_q", [P, r_passes, 2 * N], U8)
        w2_sc = kept("w2_sc", [P, r_passes, N], U8)
        w3_q = kept("w3_q", [P, m_passes, N], U32)
        w3_sc = kept("w3_sc", [P, N], U8)
        v_q = [kept("v_q%d" % a, [P, S], U32) for a in range(k_passes)]
        v_sc = kept("v_sc", [P, S], U8)
        v2_q = [kept("v2_q%d" % a, [P, PICKS], U32) for a in range(m_passes - 1)]
        v2_sc = kept("v2_sc", [P, PICKS], U8)
        h_q = {(b, c): kept("h_q%d%d" % (b, c), [P, BANK], U32) for b in range(r_passes) for c in range(halves)}
        h_sc = {key: kept("h_sc%d%d" % key, [P, BANK], U8) for key in h_q}
        y = [kept("y%d" % u, [P, S], F32) for u in range(n_tiles)]
        g = kept("g", [P, r_passes * PACK], F32)
        ward_sb = kept("ward_sb", [P, n_tiles], F32)

        def load_w1(b, a):
            rows = w1[a * PASS : (a + 1) * PASS, b * PASS : (b + 1) * PASS]
            nc.sync.dma_start(out=w1_raw[b, a][:], in_=rows.rearrange("(p i) c -> p i c", i=PACK))

        def load_words(dst, words):
            nc.sync.dma_start(out=dst[:].bitcast(I32), in_=words.rearrange("p t i -> p (t i)").bitcast(I32))

        def load_stacked_scales(dst, scales):
            passes = scales.shape[0]
            for quad in range(QUADS):
                nc.sync.dma_start(
                    out=dst[32 * quad : 32 * quad + ROWS * passes, :].bitcast(I32),
                    in_=scales[:, ROWS * quad : ROWS * (quad + 1), :].bitcast(I32))

        for plane in (tab_sc, tab2_sc, w3_sc):
            nc.vector.memset(plane[:].bitcast(I32), 0)
        nc.vector.memset(w2_sc[:].rearrange("p a n -> p (a n)").bitcast(I32), 0)

        load_w1(0, 0)
        nc.sync.dma_start(idx[:], offs)
        nc.sync.dma_start(out=g[:].rearrange("p (b t) -> p b t", t=PACK),
                          in_=gain.rearrange("(b p t) -> p b t", p=P, t=PACK))
        load_stacked_scales(tab_sc, tab_scales)
        load_w1(0, 1)
        for a in range(k_passes):
            load_words(tab[a], tab_words[a])
        for a in range(k_passes):
            load_w1(1, a)
        nc.sync.dma_start(idx2[:], offs2)
        load_stacked_scales(tab2_sc, tab2_scales)
        for a in range(m_passes - 1):
            load_words(tab2[a], tab2_words[a])
        nc.sync.dma_start(out=w2_q[:].bitcast(I32), in_=w2_words.rearrange("a p c -> p a c").bitcast(I32))
        for quad in range(QUADS):
            nc.sync.dma_start(
                out=w2_sc[32 * quad : 32 * quad + ROWS, :, :].bitcast(I32),
                in_=w2_scales[:, ROWS * quad : ROWS * (quad + 1), :].rearrange("a r n -> r a n").bitcast(I32))
        nc.sync.dma_start(out=w3_q[:].bitcast(I32), in_=w3_words.rearrange("a p c i -> p a (c i)").bitcast(I32))
        load_stacked_scales(w3_sc, w3_scales)
        load_words(tab2[m_passes - 1], tab2_words[m_passes - 1])
        nc.sync.dma_start(p1[:], pos1)
        with nc.allow_non_contiguous_dma(reason="one offset for each partition"):
            nc.sync.dma_start(out=ward_sb[:], in_=ward.rearrange("(u p) -> p u", p=P))

        sign = kept("sign", [P, r_passes * PACK], F32)
        third = kept("third", [P, r_passes * PACK], F32)
        three_g = kept("three_g", [P, r_passes * PACK], F32)
        four_g = kept("four_g", [P, r_passes * PACK], F32)
        root = kept("root", [P, r_passes * PACK], F32)
        half = kept("half", [P, r_passes * PACK], F32)
        nc.vector.memset(half[:], 0.5)
        nc.vector.tensor_scalar(sign[:], g[:], 0.0, 2.0, ALU.is_ge, ALU.mult)
        nc.vector.tensor_scalar(sign[:], sign[:], -1.0, None, ALU.add)
        nc.vector.tensor_scalar(third[:], sign[:], -1.0 / 3.0, None, ALU.mult)
        nc.vector.scalar_tensor_tensor(three_g[:], g[:], 3.0, sign[:], ALU.mult, ALU.mult)
        nc.vector.scalar_tensor_tensor(four_g[:], g[:], 4.0, sign[:], ALU.mult, ALU.mult)
        nc.gpsimd.tensor_tensor(root[:], four_g[:], half[:], ALU.pow)


        w1_bf = {}

        def round_w1(b, a, copy):
            w1_bf[b, a] = work.tile([P, PASS * PACK], BF16, name="w1_bf", align_bytes=64)
            copy(out=w1_bf[b, a][:].rearrange("p (t m i) -> p m i t", t=PACK, i=PACK),
                 in_=w1_raw[b, a][:].rearrange("p i (m t) -> p m i t", t=PACK))

        def quantise_w1(b, a):
            nc.vector.quantize_mx(out=w1_q[b, a][:].bitcast(FP8X4), scales=w1_sc[b, a][:], in_=w1_bf[b, a][:])

        def gather(dst, window, offsets, first, count):
            nc.vector.tensor_copy(dst[:, first : first + count], window[:].indirect(entries(offsets, first, count)))

        units = [(b, c) for b in range(r_passes) for c in range(halves)]
        slices = [(b, c, t) for b, c in units for t in range(PACK)]
        s_tiles, q_tiles, h_rows, h_woven = {}, {}, {}, {}

        def sine(b, c, t):
            x = ring.tile([P, BANK], F32, name="bank")
            cols = slice(c * BANK, (c + 1) * BANK)
            for a in range(k_passes):
                nc.tensor.matmul_mx(
                    out=x[:], lhsT=w1_q[b, a][:, t * P : (t + 1) * P].bitcast(FP8X4),
                    lhsT_scale=w1_sc[b, a][:, t * P : (t + 1) * P],
                    rhs=v_q[a][:, cols].bitcast(FP8X4), rhs_scale=v_sc[ROWS * a :, cols],
                    start=(a == 0), stop=(a == k_passes - 1))
            s_tiles[b, c, t] = work.tile([P, BANK], F32, name="s", bufs=6)
            col = b * PACK + t
            nc.scalar.activation(s_tiles[b, c, t][:], x[:], ACT.Sin, scale=third[:, col : col + 1])

        def square(b, c, t):
            q_tiles[b, c, t] = work.tile([P, BANK], F32, name="q", bufs=6)
            col = b * PACK + t
            nc.scalar.activation(q_tiles[b, c, t][:], s_tiles[b, c, t][:], ACT.Square, scale=root[:, col : col + 1])

        def triple(b, c, t):
            if t == 0:
                h_rows[b, c] = work.tile([P, PACK, BANK], BF16, name="h_rows", align_bytes=64)
            col = b * PACK + t
            nc.vector.scalar_tensor_tensor(h_rows[b, c][:, t, :], q_tiles[b, c, t][:], three_g[:, col : col + 1],
                                           s_tiles[b, c, t][:], ALU.subtract, ALU.mult)

        def weave(b, c):
            if (b, c) == units[-1]:
                woven = keep.tile([P, BANK * PACK], BF16, tag="last", align_bytes=64)
            else:
                woven = work.tile([P, BANK * PACK], BF16, align_bytes=64)
            h_woven[b, c] = woven
            split = BANK // 2 if (b, c) == units[-2] else 0
            for first, end, copy in ((0, split, nc.scalar.copy), (split, BANK, nc.vector.tensor_copy)):
                if end > first:
                    copy(out=woven[:, first * PACK : end * PACK].rearrange("p (j i t) -> p j t i", i=4, t=PACK),
                         in_=h_rows[b, c][:, :, first:end].rearrange("p t (j i) -> p j t i", i=4))

        def quantise_h(b, c):
            nc.vector.quantize_mx(out=h_q[b, c][:].bitcast(FP8X4), scales=h_sc[b, c][:], in_=h_woven[b, c][:])

        def second_stage(u, c):
            acc = ring.tile([P, BANK], F32, name="bank")
            for b in range(r_passes):
                nc.tensor.matmul_mx(
                    out=acc[:], lhsT=w2_q[:, b, 2 * P * u : 2 * P * (u + 1)].bitcast(FP4X4),
                    lhsT_scale=w2_sc[:, b, P * u : P * (u + 1)],
                    rhs=h_q[b, c][:].bitcast(FP8X4), rhs_scale=h_sc[b, c][:],
                    start=(b == 0), stop=(b == r_passes - 1))
            nc.scalar.copy(out=y[u][:, c * BANK : (c + 1) * BANK], in_=acc[:])

        b_banks = {}

        def prescription_pass(u, a):
            if a == 0:
                b_banks[u] = ring.tile([P, PICKS], F32, name="bank")
            nc.tensor.matmul_mx(
                out=b_banks[u][:], lhsT=w3_q[:, a, P * u : P * (u + 1)].bitcast(FP8X4),
                lhsT_scale=w3_sc[ROWS * a :, P * u : P * (u + 1)],
                rhs=v2_q[a][:].bitcast(FP8X4), rhs_scale=v2_sc[ROWS * a :, :],
                start=(a == 0), stop=(a == m_passes - 1))


        picked = [kept("picked%d" % u, [P, PICKS], F32) for u in range(n_tiles)]
        higher = [kept("higher%d" % u, [P, PICKS], F32) for u in range(n_tiles)]
        result = [kept("result%d" % u, [P, PICKS], F32) for u in range(n_tiles)]

        def join(u, first, count):
            cols = slice(first, first + count)
            nc.vector.tensor_tensor(higher[u][:, cols], b_banks[u][:, cols], picked[u][:, cols], ALU.max)
            nc.scalar.activation(result[u][:, cols], higher[u][:, cols], ACT.Identity, bias=ward_sb[:, u : u + 1])
            nc.sync.dma_start(out=out[P * u : P * (u + 1), cols], in_=result[u][:, cols])

        gather(v_sc, tab_sc, idx, 0, S)
        for a in range(k_passes):
            round_w1(0, a, nc.vector.tensor_copy)
            quantise_w1(0, a)
        gather(v_q[0], tab[0], idx, 0, S)
        for c in range(halves):
            gather(v_q[1], tab[1], idx, c * BANK, BANK)

        extras = {
            1: [lambda: round_w1(1, 0, nc.vector.tensor_copy)],
            3: [lambda: quantise_w1(1, 0)],
            5: [lambda: round_w1(1, 1, nc.scalar.copy)],
            7: [lambda: quantise_w1(1, 1), lambda: gather(v2_sc, tab2_sc, idx2, 0, PICKS)],
            9: [lambda: gather(v2_q[0], tab2[0], idx2, 0, PICKS)],
            13: [lambda: gather(v2_q[1], tab2[1], idx2, 0, PICKS)],
        }
        count = len(slices)
        for step in range(count + 4):
            if step < count:
                sine(*slices[step])
            if 0 <= step - 1 < count:
                square(*slices[step - 1])
            if 0 <= step - 2 < count:
                triple(*slices[step - 2])
            if step >= 3 and (step - 3) % PACK == PACK - 1:
                weave(*units[(step - 3) // PACK])
            if step >= 4 and (step - 4) % PACK == PACK - 1:
                quantise_h(*units[(step - 4) // PACK])
            for extra in extras.get(step, []):
                extra()
            if step == count:
                for u in range(n_tiles):
                    second_stage(u, 0)
                for u in range(n_tiles):
                    for a in range(m_passes - 1):
                        prescription_pass(u, a)
        v2_q.append(keep.tile([P, PICKS], U32, name="v2_last", tag="last", align_bytes=64))
        gather(v2_q[2], tab2[2], idx2, 0, PICKS)
        for u in range(n_tiles):
            second_stage(u, 1)
            prescription_pass(u, 2)
        last = n_tiles - 1
        for u in range(last):
            gather(picked[u], y[u], p1, 0, PICKS)
            if u > 0:
                join(u - 1, 0, PICKS)
        gather(picked[last], y[last], p1, 0, PICKS // 2)
        join(last - 1, 0, PICKS)
        gather(picked[last], y[last], p1, PICKS // 2, PICKS // 2)
        join(last, 0, PICKS // 2)
        join(last, PICKS // 2, PICKS // 2)
